import numpy as np
import ml_dtypes


def mxq(x, axis, fmt="e4m3"):
    dtype, down = {"e4m3": (ml_dtypes.float8_e4m3fn, 7), "e5m2": (ml_dtypes.float8_e5m2, 14)}[fmt]
    v = np.moveaxis(np.asarray(x, np.float32).astype(ml_dtypes.bfloat16).astype(np.float64), axis, -1)
    blocks = v.reshape(v.shape[:-1] + (-1, 32))
    amax = np.abs(blocks).max(-1, keepdims=True)
    byte = np.maximum(np.where(amax > 0, np.frexp(amax)[1] - 1 + 127, 0) - down, 1)
    scale = np.exp2(byte - 127.0)
    codes = (blocks / scale).astype(np.float32).astype(dtype).astype(np.float64)
    return np.moveaxis((codes * scale).reshape(v.shape), -1, axis)


WIDE = False


def mx_kscale(k):
    if not WIDE:
        return np.ones(k)
    levels = np.array([10, -10, 5, -5, 0])
    if k % 512:
        return np.exp2(np.random.permutation(np.resize(levels, k // 32))).repeat(32)
    a = np.empty((k // 512, 16))
    for p in range(k // 512):
        a[p, :8] = np.random.permutation(np.resize(levels, 8))
        for g in range(8):
            far = levels[np.abs(levels - a[p, g]) >= 10]
            a[p, g + 8] = far[np.random.randint(len(far))]
    return np.exp2(a.ravel()).repeat(32)


def f64(x):
    return np.asarray(x).astype(np.float64)


def striped(idx):
    return np.tile(idx.reshape(-1, 16).T, (8, 1)).astype(np.uint16)


def unstriped(offs):
    return offs[:16].T.reshape(-1).astype(np.int64)


def striped8(idx):
    return np.concatenate([x.reshape(-1, 16).T for x in idx]).astype(np.uint16)


def runs(offs, k):
    lists = np.stack([offs[16 * r : 16 * r + 16].T.reshape(-1) for r in range(8)]).astype(np.int64)
    return lists[np.arange(k) % 512 // 64]


def pack_weight(w):
    k, n = w.shape
    w = f64(np.asarray(w, np.float32).astype(ml_dtypes.bfloat16)).reshape(k // 32, 32, n)
    amax = np.abs(w).max(1)
    byte = np.clip(np.where(amax > 0, np.frexp(amax)[1] - 1 + 127 - 7, 1), 1, 254)
    scaled = (w * np.exp2(127.0 - byte)[:, None, :]).reshape(k, n).astype(np.float32)
    words = np.ascontiguousarray(scaled.reshape(k // 512, 128, 4, n).transpose(0, 1, 3, 2)).astype(ml_dtypes.float8_e4m3fn).view(np.uint8)
    return words, np.ascontiguousarray(byte.astype(np.uint8).reshape(k // 512, 16, n))


def unpack_weight(words, scales):
    g, p, n, _ = words.shape
    vals = np.ascontiguousarray(words).view(ml_dtypes.float8_e4m3fn).astype(np.float64) * np.repeat(np.exp2(scales.astype(np.float64) - 127.0), 8, axis=1)[..., None]
    return vals.transpose(0, 1, 3, 2).reshape(g * 512, n)


K, T, S, V, N, U, H = 512, 2048, 512, 1024, 512, 1024, 512


def setup_inputs():
    n = np.random.standard_normal
    s = mx_kscale(K)[:, None]
    u = mx_kscale(H)
    packed_xT = pack_weight(n((K, T)) * s)
    return {
        "x_words": packed_xT[0],
        "x_scales": packed_xT[1],
        "w1": (n((K, H)) / np.sqrt(K) / s * u).astype(np.float32),
        "mem": (n((H, U)) * u[:, None]).astype(np.float32),
        "w2": (n((H, N)) / np.sqrt(H) / u[:, None]).astype(np.float32),
        "offs": striped(np.random.permutation(T)[:S]),
        "slot": striped8(np.stack([np.random.permutation(U)[:S] for _ in range(8)])),
        "r1": striped8(np.stack([np.random.permutation(U) for _ in range(8)])),
        "r2": striped8(np.stack([np.random.permutation(U) for _ in range(8)])),
    }


def reference(x_words, x_scales, w1, mem, w2, offs, slot, r1, r2):
    xq = unpack_weight(x_words, x_scales)[:, unstriped(offs)]
    y = mxq(f64(w1), 0, "e4m3").T @ xq
    pg = f64(mem).copy()
    pg[np.arange(H)[:, None], runs(slot, H)] = y
    z = pg[np.arange(H)[:, None], runs(r1, H)] - (f64(mem)[np.arange(H)[:, None], runs(r2, H)])
    return mxq(f64(w2), 0, "e4m3").T @ mxq(z, 0, "e4m3")

@@ -1,0 +1,173 @@
+from contextlib import ExitStack
+
+import concourse.mybir as mybir
+
+K, T, S, V, N, U, H = 512, 2048, 512, 1024, 512, 1024, 512
+FLOPS = 2 * K * H * S + 2 * H * N * V
+
+F32 = mybir.dt.float32
+BF16 = mybir.dt.bfloat16
+I32 = mybir.dt.int32
+U32 = mybir.dt.uint32
+U16 = mybir.dt.uint16
+U8 = mybir.dt.uint8
+FP8X4 = mybir.dt.float8_e4m3fn_x4
+
+P = 128
+PACK = 4
+STRIPE = 16
+HALF = 512
+CHUNK = 256
+CHUNKS = V // CHUNK
+
+
+def interleave(copy, dst, src):
+    copy(
+        out=dst.rearrange("p (c i t) -> p c t i", i=4, t=PACK),
+        in_=src.rearrange("p t (c i) -> p c t i", i=4),
+    )
+
+
+def tile_picked_evictread_none_p_kernel(
+    tc, x_words, x_scales, w1, mem, w2, offs, slot, r1, r2, out
+):
+    nc = tc.nc
+    subtract = mybir.AluOpType.subtract
+    with ExitStack() as ctx:
+        lists = ctx.enter_context(tc.tile_pool(name="lists", bufs=1))
+        keep = ctx.enter_context(tc.tile_pool(name="keep", bufs=1))
+        psum = ctx.enter_context(tc.psum_pool(name="psum", bufs=1))
+
+        offs_sb = lists.tile([P, S // STRIPE], U16, name="offs_sb")
+        slot_sb = lists.tile([P, S // STRIPE], U16, name="slot_sb")
+        r1_sb = lists.tile([P, V // STRIPE], U16, name="r1_sb")
+        r2_sb = lists.tile([P, V // STRIPE], U16, name="r2_sb")
+
+        page = [keep.tile([P, U], F32, name="page%d" % t) for t in range(PACK)]
+        words = keep.tile([P, T], U32, name="words")
+        scale_rows = keep.tile([P, T], U8, name="scale_rows")
+        w1_raw = keep.tile([P, PACK, H], F32, name="w1_raw")
+        w2_raw = keep.tile([P, PACK, N], F32, name="w2_raw")
+        mem_planes = mem.rearrange("(p t) u -> t p u", t=PACK)
+
+        nc.vector.memset(scale_rows[:].bitcast(I32), 0)
+        nc.sync.dma_start(r2_sb[:], r2)
+        nc.sync.dma_start(page[0][:], mem_planes[0])
+        nc.sync.dma_start(page[1][:], mem_planes[1])
+        for q in range(4):
+            nc.sync.dma_start(
+                scale_rows[32 * q : 32 * q + 4, :].bitcast(I32),
+                x_scales[0, 4 * q : 4 * q + 4, :].bitcast(I32),
+            )
+        nc.sync.dma_start(offs_sb[:], offs)
+        nc.sync.dma_start(w1_raw[:], w1.rearrange("(p j) c -> p j c", j=PACK))
+        nc.sync.dma_start(page[2][:], mem_planes[2])
+        nc.sync.dma_start(words[:].bitcast(I32), x_words[0].rearrange("p n t -> p (n t)").bitcast(I32))
+        nc.sync.dma_start(page[3][:], mem_planes[3])
+        nc.sync.dma_start(slot_sb[:], slot)
+        nc.sync.dma_start(r1_sb[:], r1)
+        nc.sync.dma_start(w2_raw[:], w2.rearrange("(p j) c -> p j c", j=PACK))
+
+        def read_old(t, old_t):
+            for h in range(V // HALF):
+                entries = r2_sb[:, h * HALF // STRIPE : (h + 1) * HALF // STRIPE]
+                nc.vector.tensor_copy(old_t[:, h * HALF : (h + 1) * HALF], page[t][:].indirect(entries))
+
+        old = []
+        for t in range(PACK - 1):
+            old.append(keep.tile([P, V], F32, name="old%d" % t))
+            read_old(t, old[t])
+
+        x_codes = keep.tile([P, S], U32, name="x_codes", align_bytes=64)
+        x_bytes = keep.tile([P, S], U8, name="x_bytes", align_bytes=64)
+        nc.vector.tensor_copy(x_bytes[:], scale_rows[:].indirect(offs_sb[:]))
+        nc.vector.tensor_copy(x_codes[:], words[:].indirect(offs_sb[:]))
+
+        w1_bf = keep.tile([P, H * PACK], BF16, name="w1_bf", tag="w1_then_old", align_bytes=64)
+        nc.scalar.copy(
+            out=w1_bf[:].rearrange("p (t m j) -> p m j t", t=PACK, j=PACK),
+            in_=w1_raw[:].rearrange("p j (m t) -> p m j t", t=PACK),
+        )
+        w1_codes = keep.tile([P, H], U32, name="w1_codes", align_bytes=64)
+        w1_bytes = keep.tile([P, H], U8, name="w1_bytes", align_bytes=64)
+        nc.vector.quantize_mx(out=w1_codes[:].bitcast(FP8X4), scales=w1_bytes[:], in_=w1_bf[:])
+
+        old.append(keep.tile([P, V], F32, name="old_last", tag="w1_then_old", align_bytes=64))
+        read_old(PACK - 1, old[PACK - 1])
+
+        for t in range(PACK):
+            cols = slice(t * P, (t + 1) * P)
+            y_ps = psum.tile([P, S], F32, name="y_ps%d" % t)
+            nc.tensor.matmul_mx(
+                out=y_ps[:],
+                lhsT=w1_codes[:, cols].bitcast(FP8X4),
+                lhsT_scale=w1_bytes[:, cols],
+                rhs=x_codes[:].bitcast(FP8X4),
+                rhs_scale=x_bytes[:],
+                start=True,
+                stop=True,
+            )
+            y_sb = keep.tile([P, S], F32, name="y_sb%d" % t)
+            nc.scalar.copy(out=y_sb[:], in_=y_ps[:])
+            nc.vector.tensor_copy(page[t][:].indirect(slot_sb[:]), y_sb[:])
+
+        w2_bf = keep.tile([P, N * PACK], BF16, name="w2_bf", tag="w2_then_z", align_bytes=64)
+        interleave(nc.scalar.copy, w2_bf[:], w2_raw[:])
+        w2_codes = keep.tile([P, N], U32, name="w2_codes", align_bytes=64)
+        w2_bytes = keep.tile([P, N], U8, name="w2_bytes", align_bytes=64)
+        nc.vector.quantize_mx(out=w2_codes[:].bitcast(FP8X4), scales=w2_bytes[:], in_=w2_bf[:])
+
+        z_tiles = [keep.tile([P, PACK * CHUNK], F32, name="z0", tag="w2_then_z", align_bytes=64)]
+        for c in range(1, CHUNKS):
+            z_tiles.append(keep.tile([P, (PACK + 1) * CHUNK], F32, name="z%d" % c, align_bytes=64))
+        z_bf_last = keep.tile([P, PACK * CHUNK], BF16, name="z_bf_last", align_bytes=64)
+        z_bf = [z_tiles[c + 1][:, (PACK - 1) * CHUNK :].bitcast(BF16) for c in range(CHUNKS - 1)]
+        z_bf.append(z_bf_last[:])
+        out_rows = out.rearrange("(m p) v -> p m v", p=P)
+
+        def difference(c, t):
+            entries = r1_sb[:, c * CHUNK // STRIPE : (c + 1) * CHUNK // STRIPE]
+            nc.vector.tensor_tensor(
+                z_tiles[c][:, t * CHUNK : (t + 1) * CHUNK],
+                page[t][:].indirect(entries),
+                old[t][:, c * CHUNK : (c + 1) * CHUNK],
+                subtract,
+            )
+
+        def round_chunk(c):
+            copy = nc.vector.tensor_copy if c == CHUNKS - 1 else nc.scalar.copy
+            planes = z_tiles[c][:, : PACK * CHUNK].rearrange("p (t v) -> p t v", t=PACK)
+            interleave(copy, z_bf[c], planes)
+
+        def project(c):
+            z_codes = keep.tile([P, CHUNK], U32, name="z_codes%d" % c, align_bytes=64)
+            z_bytes = keep.tile([P, CHUNK], U8, name="z_bytes%d" % c, align_bytes=64)
+            nc.vector.quantize_mx(out=z_codes[:].bitcast(FP8X4), scales=z_bytes[:], in_=z_bf[c])
+            for pair in range(2):
+                o_ps = psum.tile([P, 2, CHUNK], F32, name="o_ps", tag="o_ps%d" % ((2 * c + pair) % 4))
+                for i in range(2):
+                    cols = slice((2 * pair + i) * P, (2 * pair + i + 1) * P)
+                    nc.tensor.matmul_mx(
+                        out=o_ps[:, i, :],
+                        lhsT=w2_codes[:, cols].bitcast(FP8X4),
+                        lhsT_scale=w2_bytes[:, cols],
+                        rhs=z_codes[:].bitcast(FP8X4),
+                        rhs_scale=z_bytes[:],
+                        start=True,
+                        stop=True,
+                    )
+                o_sb = keep.tile([P, 2, CHUNK], F32, name="o_sb%d_%d" % (c, pair))
+                if c == CHUNKS - 1 and pair == 1:
+                    nc.vector.tensor_copy(out=o_sb[:], in_=o_ps[:])
+                else:
+                    nc.scalar.copy(out=o_sb[:], in_=o_ps[:])
+                nc.sync.dma_start(out_rows[:, 2 * pair : 2 * pair + 2, c * CHUNK : (c + 1) * CHUNK], o_sb[:])
+
+        for c in range(CHUNKS):
+            for t in range(PACK - 1):
+                difference(c, t)
+            if c > 0:
+                project(c - 1)
+            difference(c, PACK - 1)
+            round_chunk(c)
+        project(CHUNKS - 1)

@@ -47,7 +47,7 @@ def tile_picked_evictread_none_p_kernel(
         words = keep.tile([P, T], U32, name="words")
         scale_rows = keep.tile([P, T], U8, name="scale_rows")
         w1_raw = keep.tile([P, PACK, H], F32, name="w1_raw")
-        w2_raw = keep.tile([P, PACK, N], F32, name="w2_raw")
+        w2_raw = keep.tile([P, PACK, N], F32, name="w2_raw", tag="w2_then_z")
         mem_planes = mem.rearrange("(p t) u -> t p u", t=PACK)
 
         nc.vector.memset(scale_rows[:].bitcast(I32), 0)
@@ -107,67 +107,88 @@ def tile_picked_evictread_none_p_kernel(
                 start=True,
                 stop=True,
             )
-            y_sb = keep.tile([P, S], F32, name="y_sb%d" % t)
+            y_sb = keep.tile([P, S], F32, name="y_sb", tag="y%d" % t, align_bytes=64)
             nc.scalar.copy(out=y_sb[:], in_=y_ps[:])
             nc.vector.tensor_copy(page[t][:].indirect(slot_sb[:]), y_sb[:])
 
-        w2_bf = keep.tile([P, N * PACK], BF16, name="w2_bf", tag="w2_then_z", align_bytes=64)
+        w2_bf = keep.tile([P, N * PACK], BF16, name="w2_bf", tag="y0", align_bytes=64)
         interleave(nc.scalar.copy, w2_bf[:], w2_raw[:])
         w2_codes = keep.tile([P, N], U32, name="w2_codes", align_bytes=64)
         w2_bytes = keep.tile([P, N], U8, name="w2_bytes", align_bytes=64)
         nc.vector.quantize_mx(out=w2_codes[:].bitcast(FP8X4), scales=w2_bytes[:], in_=w2_bf[:])
 
-        z_tiles = [keep.tile([P, PACK * CHUNK], F32, name="z0", tag="w2_then_z", align_bytes=64)]
-        for c in range(1, CHUNKS):
-            z_tiles.append(keep.tile([P, (PACK + 1) * CHUNK], F32, name="z%d" % c, align_bytes=64))
-        z_bf_last = keep.tile([P, PACK * CHUNK], BF16, name="z_bf_last", align_bytes=64)
-        z_bf = [z_tiles[c + 1][:, (PACK - 1) * CHUNK :].bitcast(BF16) for c in range(CHUNKS - 1)]
-        z_bf.append(z_bf_last[:])
+        z_first = keep.tile([P, 2 * PACK * CHUNK], F32, name="z_first", tag="w2_then_z")
+        z_last = keep.tile([P, PACK * CHUNK], F32, name="z_last", tag="y0", align_bytes=64)
+        z_f32 = {0: z_first[:, : PACK * CHUNK], 1: z_first[:, PACK * CHUNK :], 3: z_last[:, : PACK * CHUNK]}
+        z_bf = {1: z_last[:, : 2 * CHUNK].bitcast(BF16), 2: z_last[:, 2 * CHUNK :].bitcast(BF16)}
         out_rows = out.rearrange("(m p) v -> p m v", p=P)
 
         def difference(c, t):
             entries = r1_sb[:, c * CHUNK // STRIPE : (c + 1) * CHUNK // STRIPE]
             nc.vector.tensor_tensor(
-                z_tiles[c][:, t * CHUNK : (t + 1) * CHUNK],
+                z_f32[c][:, t * CHUNK : (t + 1) * CHUNK],
                 page[t][:].indirect(entries),
                 old[t][:, c * CHUNK : (c + 1) * CHUNK],
                 subtract,
             )
 
         def round_chunk(c):
-            copy = nc.vector.tensor_copy if c == CHUNKS - 1 else nc.scalar.copy
-            planes = z_tiles[c][:, : PACK * CHUNK].rearrange("p (t v) -> p t v", t=PACK)
-            interleave(copy, z_bf[c], planes)
+            planes = z_f32[c].rearrange("p (t v) -> p t v", t=PACK)
+            if c not in z_bf:
+                rounded = keep.tile([P, PACK * CHUNK], BF16, name="rounded", tag="z%d" % (c + 2), align_bytes=64)
+                z_bf[c] = rounded[:]
+            if c < CHUNKS - 1:
+                interleave(nc.scalar.copy, z_bf[c], planes)
+            else:
+                half = CHUNK // 2
+                interleave(nc.vector.tensor_copy, z_bf[c][:, : PACK * half], planes[:, :, :half])
+                interleave(nc.vector.tensor_copy, z_bf[c][:, PACK * half :], planes[:, :, half:])
 
         def project(c):
             z_codes = keep.tile([P, CHUNK], U32, name="z_codes%d" % c, align_bytes=64)
             z_bytes = keep.tile([P, CHUNK], U8, name="z_bytes%d" % c, align_bytes=64)
-            nc.vector.quantize_mx(out=z_codes[:].bitcast(FP8X4), scales=z_bytes[:], in_=z_bf[c])
-            for pair in range(2):
-                o_ps = psum.tile([P, 2, CHUNK], F32, name="o_ps", tag="o_ps%d" % ((2 * c + pair) % 4))
-                for i in range(2):
-                    cols = slice((2 * pair + i) * P, (2 * pair + i + 1) * P)
+            pieces = 2 if c == CHUNKS - 1 else 1
+            per_bank = 2 // pieces
+            width = CHUNK // pieces
+            banks = {}
+            for first in range(0, N // P, per_bank):
+                tag = "y_ps%d" % first if per_bank == 1 else "o_ps%d" % ((2 * c + first // 2) % 4)
+                banks[first] = psum.tile([P, per_bank, CHUNK], F32, name="o_ps", tag=tag)
+            for piece in range(pieces):
+                vs = slice(piece * width, (piece + 1) * width)
+                nc.vector.quantize_mx(
+                    out=z_codes[:, vs].bitcast(FP8X4),
+                    scales=z_bytes[:, vs],
+                    in_=z_bf[c][:, PACK * vs.start : PACK * vs.stop],
+                )
+                for m in range(N // P):
+                    cols = slice(m * P, (m + 1) * P)
                     nc.tensor.matmul_mx(
-                        out=o_ps[:, i, :],
+                        out=banks[m - m % per_bank][:, m % per_bank, vs],
                         lhsT=w2_codes[:, cols].bitcast(FP8X4),
                         lhsT_scale=w2_bytes[:, cols],
-                        rhs=z_codes[:].bitcast(FP8X4),
-                        rhs_scale=z_bytes[:],
+                        rhs=z_codes[:, vs].bitcast(FP8X4),
+                        rhs_scale=z_bytes[:, vs],
                         start=True,
                         stop=True,
                     )
-                o_sb = keep.tile([P, 2, CHUNK], F32, name="o_sb%d_%d" % (c, pair))
-                if c == CHUNKS - 1 and pair == 1:
+            for first, o_ps in banks.items():
+                o_sb = keep.tile([P, per_bank, CHUNK], F32, name="o_sb%d_%d" % (c, first))
+                if per_bank == 1 and first % 2 == 1:
                     nc.vector.tensor_copy(out=o_sb[:], in_=o_ps[:])
                 else:
                     nc.scalar.copy(out=o_sb[:], in_=o_ps[:])
-                nc.sync.dma_start(out_rows[:, 2 * pair : 2 * pair + 2, c * CHUNK : (c + 1) * CHUNK], o_sb[:])
+                nc.sync.dma_start(out_rows[:, first : first + per_bank, c * CHUNK : (c + 1) * CHUNK], o_sb[:])
 
         for c in range(CHUNKS):
-            for t in range(PACK - 1):
+            if c >= 2:
+                project(c - 2)
+            if c == 2:
+                fresh = keep.tile([P, PACK * CHUNK], F32, name="fresh", tag="z%d" % c, align_bytes=64)
+                z_f32[c] = fresh[:]
+            for t in range(PACK):
+                if c == CHUNKS - 1 and t == 2:
+                    project(c - 1)
                 difference(c, t)
-            if c > 0:
-                project(c - 1)
-            difference(c, PACK - 1)
             round_chunk(c)
         project(CHUNKS - 1)

@@ -46,8 +46,8 @@ def tile_picked_evictread_none_p_kernel(
         page = [keep.tile([P, U], F32, name="page%d" % t) for t in range(PACK)]
         words = keep.tile([P, T], U32, name="words")
         scale_rows = keep.tile([P, T], U8, name="scale_rows")
-        w1_raw = keep.tile([P, PACK, H], F32, name="w1_raw")
-        w2_raw = keep.tile([P, PACK, N], F32, name="w2_raw", tag="w2_then_z")
+        w1_raw = keep.tile([P, PACK, H], F32, name="w1_raw", tag="w1_raw_then_old", align_bytes=64)
+        w2_raw = keep.tile([P, PACK, N], F32, name="w2_raw", tag="w2_then_z", align_bytes=64)
         mem_planes = mem.rearrange("(p t) u -> t p u", t=PACK)
 
         nc.vector.memset(scale_rows[:].bitcast(I32), 0)
@@ -68,15 +68,16 @@ def tile_picked_evictread_none_p_kernel(
         nc.sync.dma_start(r1_sb[:], r1)
         nc.sync.dma_start(w2_raw[:], w2.rearrange("(p j) c -> p j c", j=PACK))
 
-        def read_old(t, old_t):
-            for h in range(V // HALF):
-                entries = r2_sb[:, h * HALF // STRIPE : (h + 1) * HALF // STRIPE]
-                nc.vector.tensor_copy(old_t[:, h * HALF : (h + 1) * HALF], page[t][:].indirect(entries))
+        old = {}
 
-        old = []
+        def read_old(t, h, tag):
+            old[t, h] = keep.tile([P, HALF], F32, name="old", tag=tag, align_bytes=64)
+            entries = r2_sb[:, h * HALF // STRIPE : (h + 1) * HALF // STRIPE]
+            nc.vector.tensor_copy(old[t, h][:], page[t][:].indirect(entries))
+
         for t in range(PACK - 1):
-            old.append(keep.tile([P, V], F32, name="old%d" % t))
-            read_old(t, old[t])
+            for h in range(V // HALF):
+                read_old(t, h, "old%d_%d" % (t, h))
 
         x_codes = keep.tile([P, S], U32, name="x_codes", align_bytes=64)
         x_bytes = keep.tile([P, S], U8, name="x_bytes", align_bytes=64)
@@ -92,8 +93,8 @@ def tile_picked_evictread_none_p_kernel(
         w1_bytes = keep.tile([P, H], U8, name="w1_bytes", align_bytes=64)
         nc.vector.quantize_mx(out=w1_codes[:].bitcast(FP8X4), scales=w1_bytes[:], in_=w1_bf[:])
 
-        old.append(keep.tile([P, V], F32, name="old_last", tag="w1_then_old", align_bytes=64))
-        read_old(PACK - 1, old[PACK - 1])
+        read_old(PACK - 1, 0, "w1_raw_then_old")
+        read_old(PACK - 1, 1, "w1_then_old")
 
         for t in range(PACK):
             cols = slice(t * P, (t + 1) * P)
@@ -117,23 +118,23 @@ def tile_picked_evictread_none_p_kernel(
         w2_bytes = keep.tile([P, N], U8, name="w2_bytes", align_bytes=64)
         nc.vector.quantize_mx(out=w2_codes[:].bitcast(FP8X4), scales=w2_bytes[:], in_=w2_bf[:])
 
-        z_first = keep.tile([P, 2 * PACK * CHUNK], F32, name="z_first", tag="w2_then_z")
-        z_last = keep.tile([P, PACK * CHUNK], F32, name="z_last", tag="y0", align_bytes=64)
-        z_f32 = {0: z_first[:, : PACK * CHUNK], 1: z_first[:, PACK * CHUNK :], 3: z_last[:, : PACK * CHUNK]}
-        z_bf = {1: z_last[:, : 2 * CHUNK].bitcast(BF16), 2: z_last[:, 2 * CHUNK :].bitcast(BF16)}
+        z_space = keep.tile([P, 15, CHUNK], F32, name="z_space", tag="w2_then_z", align_bytes=64)
+        z_f32 = [z_space[:, 5:9, :], z_space[:, 0:4, :], z_space[:, 8:12, :], z_space[:, 3:15:3, :]]
+        z_flat = z_space[:].rearrange("p b v -> p (b v)")
+        z_bf = {c: z_flat[:, b * CHUNK : (b + 2) * CHUNK].bitcast(BF16) for c, b in enumerate((9, 5, 12))}
         out_rows = out.rearrange("(m p) v -> p m v", p=P)
 
         def difference(c, t):
             entries = r1_sb[:, c * CHUNK // STRIPE : (c + 1) * CHUNK // STRIPE]
             nc.vector.tensor_tensor(
-                z_f32[c][:, t * CHUNK : (t + 1) * CHUNK],
+                z_f32[c][:, t, :],
                 page[t][:].indirect(entries),
-                old[t][:, c * CHUNK : (c + 1) * CHUNK],
+                old[t, c * CHUNK // HALF][:, c * CHUNK % HALF : c * CHUNK % HALF + CHUNK],
                 subtract,
             )
 
         def round_chunk(c):
-            planes = z_f32[c].rearrange("p (t v) -> p t v", t=PACK)
+            planes = z_f32[c]
             if c not in z_bf:
                 rounded = keep.tile([P, PACK * CHUNK], BF16, name="rounded", tag="z%d" % (c + 2), align_bytes=64)
                 z_bf[c] = rounded[:]
@@ -183,9 +184,6 @@ def tile_picked_evictread_none_p_kernel(
         for c in range(CHUNKS):
             if c >= 2:
                 project(c - 2)
-            if c == 2:
-                fresh = keep.tile([P, PACK * CHUNK], F32, name="fresh", tag="z%d" % c, align_bytes=64)
-                z_f32[c] = fresh[:]
             for t in range(PACK):
                 if c == CHUNKS - 1 and t == 2:
                     project(c - 1)

@@ -15,16 +15,43 @@ FP8X4 = mybir.dt.float8_e4m3fn_x4
 
 P = 128
 PACK = 4
+QUADRANT = 32
 STRIPE = 16
-HALF = 512
-CHUNK = 256
+RUN = 4
+ALIGN = 64
+HALF = V // 2
+CHUNK = V // 4
 CHUNKS = V // CHUNK
+LAST = CHUNKS - 1
+ROW_TILES = N // P
+
+Z_BLOCKS = 12
+Z_PLANE_BLOCKS = (slice(0, 4), slice(6, 10), slice(3, 7), slice(2, 12, 3))
+Z_ROUNDED_BLOCK = (4, 1, 10)
+LAST_PLANE_ORDER = (2, 0, 1, 3)
 
 
 def interleave(copy, dst, src):
     copy(
-        out=dst.rearrange("p (c i t) -> p c t i", i=4, t=PACK),
-        in_=src.rearrange("p t (c i) -> p c t i", i=4),
+        out=dst.rearrange("p (c i t) -> p c t i", i=RUN, t=PACK),
+        in_=src.rearrange("p t (c i) -> p c t i", i=RUN),
+    )
+
+
+def entries(list_tile, first, count):
+    return list_tile[:, first // STRIPE : (first + count) // STRIPE]
+
+
+def product(nc, acc, w_codes, w_bytes, m, codes, scale_bytes):
+    cols = slice(m * P, (m + 1) * P)
+    nc.tensor.matmul_mx(
+        out=acc,
+        lhsT=w_codes[:, cols].bitcast(FP8X4),
+        lhsT_scale=w_bytes[:, cols],
+        rhs=codes.bitcast(FP8X4),
+        rhs_scale=scale_bytes,
+        start=True,
+        stop=True,
     )
 
 
@@ -32,7 +59,6 @@ def tile_picked_evictread_none_p_kernel(
     tc, x_words, x_scales, w1, mem, w2, offs, slot, r1, r2, out
 ):
     nc = tc.nc
-    subtract = mybir.AluOpType.subtract
     with ExitStack() as ctx:
         lists = ctx.enter_context(tc.tile_pool(name="lists", bufs=1))
         keep = ctx.enter_context(tc.tile_pool(name="keep", bufs=1))
@@ -46,23 +72,24 @@ def tile_picked_evictread_none_p_kernel(
         page = [keep.tile([P, U], F32, name="page%d" % t) for t in range(PACK)]
         words = keep.tile([P, T], U32, name="words")
         scale_rows = keep.tile([P, T], U8, name="scale_rows")
-        w1_raw = keep.tile([P, PACK, H], F32, name="w1_raw", tag="w1_raw_then_old", align_bytes=64)
-        w2_raw = keep.tile([P, PACK, N], F32, name="w2_raw", tag="w2_then_z", align_bytes=64)
+        w1_raw = keep.tile([P, PACK, H], F32, name="w1_raw", tag="w1_raw", align_bytes=ALIGN)
+        w2_raw = keep.tile([P, PACK, N], F32, name="w2_raw", tag="w2_raw", align_bytes=ALIGN)
         mem_planes = mem.rearrange("(p t) u -> t p u", t=PACK)
 
         nc.vector.memset(scale_rows[:].bitcast(I32), 0)
-        nc.sync.dma_start(r2_sb[:], r2)
+
         nc.sync.dma_start(page[0][:], mem_planes[0])
+        nc.sync.dma_start(r2_sb[:], r2)
         nc.sync.dma_start(page[1][:], mem_planes[1])
-        for q in range(4):
+        for q in range(P // QUADRANT):
             nc.sync.dma_start(
-                scale_rows[32 * q : 32 * q + 4, :].bitcast(I32),
-                x_scales[0, 4 * q : 4 * q + 4, :].bitcast(I32),
+                scale_rows[QUADRANT * q : QUADRANT * q + PACK, :].bitcast(I32),
+                x_scales[0, PACK * q : PACK * (q + 1), :].bitcast(I32),
             )
         nc.sync.dma_start(offs_sb[:], offs)
         nc.sync.dma_start(w1_raw[:], w1.rearrange("(p j) c -> p j c", j=PACK))
         nc.sync.dma_start(page[2][:], mem_planes[2])
-        nc.sync.dma_start(words[:].bitcast(I32), x_words[0].rearrange("p n t -> p (n t)").bitcast(I32))
+        nc.sync.dma_start(words[:].bitcast(I32), x_words[0].rearrange("p n j -> p (n j)").bitcast(I32))
         nc.sync.dma_start(page[3][:], mem_planes[3])
         nc.sync.dma_start(slot_sb[:], slot)
         nc.sync.dma_start(r1_sb[:], r1)
@@ -71,122 +98,110 @@ def tile_picked_evictread_none_p_kernel(
         old = {}
 
         def read_old(t, h, tag):
-            old[t, h] = keep.tile([P, HALF], F32, name="old", tag=tag, align_bytes=64)
-            entries = r2_sb[:, h * HALF // STRIPE : (h + 1) * HALF // STRIPE]
-            nc.vector.tensor_copy(old[t, h][:], page[t][:].indirect(entries))
+            old[t, h] = keep.tile([P, HALF], F32, name="old", tag=tag, align_bytes=ALIGN)
+            nc.vector.tensor_copy(old[t, h][:], page[t][:].indirect(entries(r2_sb, h * HALF, HALF)))
 
         for t in range(PACK - 1):
             for h in range(V // HALF):
                 read_old(t, h, "old%d_%d" % (t, h))
 
-        x_codes = keep.tile([P, S], U32, name="x_codes", align_bytes=64)
-        x_bytes = keep.tile([P, S], U8, name="x_bytes", align_bytes=64)
+        x_codes = keep.tile([P, S], U32, name="x_codes", align_bytes=ALIGN)
+        x_bytes = keep.tile([P, S], U8, name="x_bytes", align_bytes=ALIGN)
         nc.vector.tensor_copy(x_bytes[:], scale_rows[:].indirect(offs_sb[:]))
         nc.vector.tensor_copy(x_codes[:], words[:].indirect(offs_sb[:]))
 
-        w1_bf = keep.tile([P, H * PACK], BF16, name="w1_bf", tag="w1_then_old", align_bytes=64)
+        w1_bf = keep.tile([P, H * PACK], BF16, name="w1_bf", tag="w1_bf", align_bytes=ALIGN)
         nc.scalar.copy(
             out=w1_bf[:].rearrange("p (t m j) -> p m j t", t=PACK, j=PACK),
             in_=w1_raw[:].rearrange("p j (m t) -> p m j t", t=PACK),
         )
-        w1_codes = keep.tile([P, H], U32, name="w1_codes", align_bytes=64)
-        w1_bytes = keep.tile([P, H], U8, name="w1_bytes", align_bytes=64)
+        w1_codes = keep.tile([P, H], U32, name="w1_codes", align_bytes=ALIGN)
+        w1_bytes = keep.tile([P, H], U8, name="w1_bytes", align_bytes=ALIGN)
         nc.vector.quantize_mx(out=w1_codes[:].bitcast(FP8X4), scales=w1_bytes[:], in_=w1_bf[:])
 
-        read_old(PACK - 1, 0, "w1_raw_then_old")
-        read_old(PACK - 1, 1, "w1_then_old")
+        read_old(PACK - 1, 0, "w1_raw")
+        read_old(PACK - 1, 1, "w1_bf")
 
         for t in range(PACK):
-            cols = slice(t * P, (t + 1) * P)
-            y_ps = psum.tile([P, S], F32, name="y_ps%d" % t)
-            nc.tensor.matmul_mx(
-                out=y_ps[:],
-                lhsT=w1_codes[:, cols].bitcast(FP8X4),
-                lhsT_scale=w1_bytes[:, cols],
-                rhs=x_codes[:].bitcast(FP8X4),
-                rhs_scale=x_bytes[:],
-                start=True,
-                stop=True,
-            )
-            y_sb = keep.tile([P, S], F32, name="y_sb", tag="y%d" % t, align_bytes=64)
+            y_ps = psum.tile([P, S], F32, name="y_ps", tag="bank%d" % t)
+            product(nc, y_ps[:], w1_codes, w1_bytes, t, x_codes[:], x_bytes[:])
+            y_sb = keep.tile([P, S], F32, name="y_sb", tag="y%d" % t, align_bytes=ALIGN)
             nc.scalar.copy(out=y_sb[:], in_=y_ps[:])
             nc.vector.tensor_copy(page[t][:].indirect(slot_sb[:]), y_sb[:])
 
-        w2_bf = keep.tile([P, N * PACK], BF16, name="w2_bf", tag="y0", align_bytes=64)
+        w2_bf = keep.tile([P, N * PACK], BF16, name="w2_bf", tag="y0", align_bytes=ALIGN)
         interleave(nc.scalar.copy, w2_bf[:], w2_raw[:])
-        w2_codes = keep.tile([P, N], U32, name="w2_codes", align_bytes=64)
-        w2_bytes = keep.tile([P, N], U8, name="w2_bytes", align_bytes=64)
+        w2_codes = keep.tile([P, N], U32, name="w2_codes", align_bytes=ALIGN)
+        w2_bytes = keep.tile([P, N], U8, name="w2_bytes", align_bytes=ALIGN)
         nc.vector.quantize_mx(out=w2_codes[:].bitcast(FP8X4), scales=w2_bytes[:], in_=w2_bf[:])
 
-        z_space = keep.tile([P, 15, CHUNK], F32, name="z_space", tag="w2_then_z", align_bytes=64)
-        z_f32 = [z_space[:, 5:9, :], z_space[:, 0:4, :], z_space[:, 8:12, :], z_space[:, 3:15:3, :]]
+        z_space = keep.tile([P, Z_BLOCKS, CHUNK], F32, name="z_space", tag="w2_raw", align_bytes=ALIGN)
         z_flat = z_space[:].rearrange("p b v -> p (b v)")
-        z_bf = {c: z_flat[:, b * CHUNK : (b + 2) * CHUNK].bitcast(BF16) for c, b in enumerate((9, 5, 12))}
+        z_last_bf = keep.tile([P, PACK * CHUNK], BF16, name="z_last_bf", align_bytes=ALIGN)
+        z_planes = [z_space[:, blocks, :] for blocks in Z_PLANE_BLOCKS]
+        z_bf = [z_flat[:, b * CHUNK : (b + 2) * CHUNK].bitcast(BF16) for b in Z_ROUNDED_BLOCK] + [z_last_bf[:]]
         out_rows = out.rearrange("(m p) v -> p m v", p=P)
 
         def difference(c, t):
-            entries = r1_sb[:, c * CHUNK // STRIPE : (c + 1) * CHUNK // STRIPE]
+            h, first = divmod(c * CHUNK, HALF)
             nc.vector.tensor_tensor(
-                z_f32[c][:, t, :],
-                page[t][:].indirect(entries),
-                old[t, c * CHUNK // HALF][:, c * CHUNK % HALF : c * CHUNK % HALF + CHUNK],
-                subtract,
+                z_planes[c][:, t, :],
+                page[t][:].indirect(entries(r1_sb, c * CHUNK, CHUNK)),
+                old[t, h][:, first : first + CHUNK],
+                mybir.AluOpType.subtract,
             )
 
-        def round_chunk(c):
-            planes = z_f32[c]
-            if c not in z_bf:
-                rounded = keep.tile([P, PACK * CHUNK], BF16, name="rounded", tag="z%d" % (c + 2), align_bytes=64)
-                z_bf[c] = rounded[:]
-            if c < CHUNKS - 1:
-                interleave(nc.scalar.copy, z_bf[c], planes)
-            else:
-                half = CHUNK // 2
-                interleave(nc.vector.tensor_copy, z_bf[c][:, : PACK * half], planes[:, :, :half])
-                interleave(nc.vector.tensor_copy, z_bf[c][:, PACK * half :], planes[:, :, half:])
+        def quantised_tiles(c):
+            z_codes = keep.tile([P, CHUNK], U32, name="z_codes%d" % c, align_bytes=ALIGN)
+            z_bytes = keep.tile([P, CHUNK], U8, name="z_bytes%d" % c, align_bytes=ALIGN)
+            return z_codes, z_bytes
 
         def project(c):
-            z_codes = keep.tile([P, CHUNK], U32, name="z_codes%d" % c, align_bytes=64)
-            z_bytes = keep.tile([P, CHUNK], U8, name="z_bytes%d" % c, align_bytes=64)
-            pieces = 2 if c == CHUNKS - 1 else 1
-            per_bank = 2 // pieces
-            width = CHUNK // pieces
-            banks = {}
-            for first in range(0, N // P, per_bank):
-                tag = "y_ps%d" % first if per_bank == 1 else "o_ps%d" % ((2 * c + first // 2) % 4)
-                banks[first] = psum.tile([P, per_bank, CHUNK], F32, name="o_ps", tag=tag)
-            for piece in range(pieces):
-                vs = slice(piece * width, (piece + 1) * width)
-                nc.vector.quantize_mx(
-                    out=z_codes[:, vs].bitcast(FP8X4),
-                    scales=z_bytes[:, vs],
-                    in_=z_bf[c][:, PACK * vs.start : PACK * vs.stop],
-                )
-                for m in range(N // P):
-                    cols = slice(m * P, (m + 1) * P)
-                    nc.tensor.matmul_mx(
-                        out=banks[m - m % per_bank][:, m % per_bank, vs],
-                        lhsT=w2_codes[:, cols].bitcast(FP8X4),
-                        lhsT_scale=w2_bytes[:, cols],
-                        rhs=z_codes[:, vs].bitcast(FP8X4),
-                        rhs_scale=z_bytes[:, vs],
-                        start=True,
-                        stop=True,
-                    )
-            for first, o_ps in banks.items():
-                o_sb = keep.tile([P, per_bank, CHUNK], F32, name="o_sb%d_%d" % (c, first))
-                if per_bank == 1 and first % 2 == 1:
-                    nc.vector.tensor_copy(out=o_sb[:], in_=o_ps[:])
-                else:
-                    nc.scalar.copy(out=o_sb[:], in_=o_ps[:])
-                nc.sync.dma_start(out_rows[:, first : first + per_bank, c * CHUNK : (c + 1) * CHUNK], o_sb[:])
+            z_codes, z_bytes = quantised_tiles(c)
+            nc.vector.quantize_mx(out=z_codes[:].bitcast(FP8X4), scales=z_bytes[:], in_=z_bf[c])
+            banks = [
+                psum.tile([P, 2, CHUNK], F32, name="acc", tag="bank%d" % (PACK + (2 * c + pair) % 4))
+                for pair in range(ROW_TILES // 2)
+            ]
+            for m in range(ROW_TILES):
+                product(nc, banks[m // 2][:, m % 2, :], w2_codes, w2_bytes, m, z_codes[:], z_bytes[:])
+            for pair, acc in enumerate(banks):
+                staged = keep.tile([P, 2, CHUNK], F32, name="staged%d_%d" % (c, 2 * pair))
+                nc.scalar.copy(out=staged[:], in_=acc[:])
+                nc.sync.dma_start(out_rows[:, 2 * pair : 2 * pair + 2, c * CHUNK : (c + 1) * CHUNK], staged[:])
 
-        for c in range(CHUNKS):
+        def finish_last():
+            width = CHUNK // 2
+            halves = [slice(0, width), slice(width, CHUNK)]
+            rounded = [z_bf[LAST][:, PACK * cols.start : PACK * cols.stop] for cols in halves]
+            for cols, dst in zip(halves, rounded):
+                interleave(nc.vector.tensor_copy, dst, z_planes[LAST][:, :, cols])
+            z_codes, z_bytes = quantised_tiles(LAST)
+            banks = {}
+            for half, (cols, src) in enumerate(zip(halves, rounded)):
+                nc.vector.quantize_mx(out=z_codes[:, cols].bitcast(FP8X4), scales=z_bytes[:, cols], in_=src)
+                for m in range(ROW_TILES):
+                    banks[half, m] = psum.tile([P, width], F32, name="acc", tag="bank%d" % (ROW_TILES * half + m))
+                    product(nc, banks[half, m][:], w2_codes, w2_bytes, m, z_codes[:, cols], z_bytes[:, cols])
+            for half, cols in enumerate(halves):
+                first = LAST * CHUNK + cols.start
+                for m in range(0, ROW_TILES, 2):
+                    staged = keep.tile([P, 2, width], F32, name="staged_last%d_%d" % (half, m))
+                    nc.scalar.copy(out=staged[:, 0, :], in_=banks[half, m][:])
+                    nc.vector.tensor_copy(out=staged[:, 1, :], in_=banks[half, m + 1][:])
+                    nc.sync.dma_start(out_rows[:, m : m + 2, first : first + width], staged[:])
+
+        for c in range(LAST):
             if c >= 2:
                 project(c - 2)
             for t in range(PACK):
-                if c == CHUNKS - 1 and t == 2:
-                    project(c - 1)
                 difference(c, t)
-            round_chunk(c)
-        project(CHUNKS - 1)
+            interleave(nc.scalar.copy, z_bf[c], z_planes[c])
+
+        project(LAST - 2)
+        for t in LAST_PLANE_ORDER[:2]:
+            difference(LAST, t)
+        project(LAST - 1)
+        for t in LAST_PLANE_ORDER[2:]:
+            difference(LAST, t)
+        finish_last()

from contextlib import ExitStack

import concourse.mybir as mybir

K, T, S, V, N, U, H = 512, 2048, 512, 1024, 512, 1024, 512
FLOPS = 2 * K * H * S + 2 * H * N * V

F32 = mybir.dt.float32
BF16 = mybir.dt.bfloat16
I32 = mybir.dt.int32
U32 = mybir.dt.uint32
U16 = mybir.dt.uint16
U8 = mybir.dt.uint8
FP8X4 = mybir.dt.float8_e4m3fn_x4

P = 128
PACK = 4
QUADRANT = 32
STRIPE = 16
RUN = 4
ALIGN = 64
HALF = V // 2
CHUNK = V // 4
CHUNKS = V // CHUNK
LAST = CHUNKS - 1
ROW_TILES = N // P

Z_BLOCKS = 12
Z_PLANE_BLOCKS = (slice(0, 4), slice(6, 10), slice(3, 7), slice(2, 12, 3))
Z_ROUNDED_BLOCK = (4, 1, 10)
LAST_PLANE_ORDER = (2, 0, 1, 3)


def interleave(copy, dst, src):
    copy(
        out=dst.rearrange("p (c i t) -> p c t i", i=RUN, t=PACK),
        in_=src.rearrange("p t (c i) -> p c t i", i=RUN),
    )


def entries(list_tile, first, count):
    return list_tile[:, first // STRIPE : (first + count) // STRIPE]


def product(nc, acc, w_codes, w_bytes, m, codes, scale_bytes):
    cols = slice(m * P, (m + 1) * P)
    nc.tensor.matmul_mx(
        out=acc,
        lhsT=w_codes[:, cols].bitcast(FP8X4),
        lhsT_scale=w_bytes[:, cols],
        rhs=codes.bitcast(FP8X4),
        rhs_scale=scale_bytes,
        start=True,
        stop=True,
    )


def tile_picked_evictread_none_p_kernel(
    tc, x_words, x_scales, w1, mem, w2, offs, slot, r1, r2, out
):
    nc = tc.nc
    with ExitStack() as ctx:
        lists = ctx.enter_context(tc.tile_pool(name="lists", bufs=1))
        keep = ctx.enter_context(tc.tile_pool(name="keep", bufs=1))
        psum = ctx.enter_context(tc.psum_pool(name="psum", bufs=1))

        offs_sb = lists.tile([P, S // STRIPE], U16, name="offs_sb")
        slot_sb = lists.tile([P, S // STRIPE], U16, name="slot_sb")
        r1_sb = lists.tile([P, V // STRIPE], U16, name="r1_sb")
        r2_sb = lists.tile([P, V // STRIPE], U16, name="r2_sb")

        page = [keep.tile([P, U], F32, name="page%d" % t) for t in range(PACK)]
        words = keep.tile([P, T], U32, name="words")
        scale_rows = keep.tile([P, T], U8, name="scale_rows")
        w1_raw = keep.tile([P, PACK, H], F32, name="w1_raw", tag="w1_raw", align_bytes=ALIGN)
        w2_raw = keep.tile([P, PACK, N], F32, name="w2_raw", tag="w2_raw", align_bytes=ALIGN)
        mem_planes = mem.rearrange("(p t) u -> t p u", t=PACK)

        nc.vector.memset(scale_rows[:].bitcast(I32), 0)

        nc.sync.dma_start(page[0][:], mem_planes[0])
        nc.sync.dma_start(r2_sb[:], r2)
        nc.sync.dma_start(page[1][:], mem_planes[1])
        for q in range(P // QUADRANT):
            nc.sync.dma_start(
                scale_rows[QUADRANT * q : QUADRANT * q + PACK, :].bitcast(I32),
                x_scales[0, PACK * q : PACK * (q + 1), :].bitcast(I32),
            )
        nc.sync.dma_start(offs_sb[:], offs)
        nc.sync.dma_start(w1_raw[:], w1.rearrange("(p j) c -> p j c", j=PACK))
        nc.sync.dma_start(page[2][:], mem_planes[2])
        nc.sync.dma_start(words[:].bitcast(I32), x_words[0].rearrange("p n j -> p (n j)").bitcast(I32))
        nc.sync.dma_start(page[3][:], mem_planes[3])
        nc.sync.dma_start(slot_sb[:], slot)
        nc.sync.dma_start(r1_sb[:], r1)
        nc.sync.dma_start(w2_raw[:], w2.rearrange("(p j) c -> p j c", j=PACK))

        old = {}

        def read_old(t, h, tag):
            old[t, h] = keep.tile([P, HALF], F32, name="old", tag=tag, align_bytes=ALIGN)
            nc.vector.tensor_copy(old[t, h][:], page[t][:].indirect(entries(r2_sb, h * HALF, HALF)))

        for t in range(PACK - 1):
            for h in range(V // HALF):
                read_old(t, h, "old%d_%d" % (t, h))

        x_codes = keep.tile([P, S], U32, name="x_codes", align_bytes=ALIGN)
        x_bytes = keep.tile([P, S], U8, name="x_bytes", align_bytes=ALIGN)
        nc.vector.tensor_copy(x_bytes[:], scale_rows[:].indirect(offs_sb[:]))
        nc.vector.tensor_copy(x_codes[:], words[:].indirect(offs_sb[:]))

        w1_bf = keep.tile([P, H * PACK], BF16, name="w1_bf", tag="w1_bf", align_bytes=ALIGN)
        nc.scalar.copy(
            out=w1_bf[:].rearrange("p (t m j) -> p m j t", t=PACK, j=PACK),
            in_=w1_raw[:].rearrange("p j (m t) -> p m j t", t=PACK),
        )
        w1_codes = keep.tile([P, H], U32, name="w1_codes", align_bytes=ALIGN)
        w1_bytes = keep.tile([P, H], U8, name="w1_bytes", align_bytes=ALIGN)
        nc.vector.quantize_mx(out=w1_codes[:].bitcast(FP8X4), scales=w1_bytes[:], in_=w1_bf[:])

        read_old(PACK - 1, 0, "w1_raw")
        read_old(PACK - 1, 1, "w1_bf")

        for t in range(PACK):
            y_ps = psum.tile([P, S], F32, name="y_ps", tag="bank%d" % t)
            product(nc, y_ps[:], w1_codes, w1_bytes, t, x_codes[:], x_bytes[:])
            y_sb = keep.tile([P, S], F32, name="y_sb", tag="y%d" % t, align_bytes=ALIGN)
            nc.scalar.copy(out=y_sb[:], in_=y_ps[:])
            nc.vector.tensor_copy(page[t][:].indirect(slot_sb[:]), y_sb[:])

        w2_bf = keep.tile([P, N * PACK], BF16, name="w2_bf", tag="y0", align_bytes=ALIGN)
        interleave(nc.scalar.copy, w2_bf[:], w2_raw[:])
        w2_codes = keep.tile([P, N], U32, name="w2_codes", align_bytes=ALIGN)
        w2_bytes = keep.tile([P, N], U8, name="w2_bytes", align_bytes=ALIGN)
        nc.vector.quantize_mx(out=w2_codes[:].bitcast(FP8X4), scales=w2_bytes[:], in_=w2_bf[:])

        z_space = keep.tile([P, Z_BLOCKS, CHUNK], F32, name="z_space", tag="w2_raw", align_bytes=ALIGN)
        z_flat = z_space[:].rearrange("p b v -> p (b v)")
        z_last_bf = keep.tile([P, PACK * CHUNK], BF16, name="z_last_bf", align_bytes=ALIGN)
        z_planes = [z_space[:, blocks, :] for blocks in Z_PLANE_BLOCKS]
        z_bf = [z_flat[:, b * CHUNK : (b + 2) * CHUNK].bitcast(BF16) for b in Z_ROUNDED_BLOCK] + [z_last_bf[:]]
        out_rows = out.rearrange("(m p) v -> p m v", p=P)

        def difference(c, t):
            h, first = divmod(c * CHUNK, HALF)
            nc.vector.tensor_tensor(
                z_planes[c][:, t, :],
                page[t][:].indirect(entries(r1_sb, c * CHUNK, CHUNK)),
                old[t, h][:, first : first + CHUNK],
                mybir.AluOpType.subtract,
            )

        def quantised_tiles(c):
            z_codes = keep.tile([P, CHUNK], U32, name="z_codes%d" % c, align_bytes=ALIGN)
            z_bytes = keep.tile([P, CHUNK], U8, name="z_bytes%d" % c, align_bytes=ALIGN)
            return z_codes, z_bytes

        def project(c):
            z_codes, z_bytes = quantised_tiles(c)
            nc.vector.quantize_mx(out=z_codes[:].bitcast(FP8X4), scales=z_bytes[:], in_=z_bf[c])
            banks = [
                psum.tile([P, 2, CHUNK], F32, name="acc", tag="bank%d" % (PACK + (2 * c + pair) % 4))
                for pair in range(ROW_TILES // 2)
            ]
            for m in range(ROW_TILES):
                product(nc, banks[m // 2][:, m % 2, :], w2_codes, w2_bytes, m, z_codes[:], z_bytes[:])
            for pair, acc in enumerate(banks):
                staged = keep.tile([P, 2, CHUNK], F32, name="staged%d_%d" % (c, 2 * pair))
                nc.scalar.copy(out=staged[:], in_=acc[:])
                nc.sync.dma_start(out_rows[:, 2 * pair : 2 * pair + 2, c * CHUNK : (c + 1) * CHUNK], staged[:])

        def finish_last():
            width = CHUNK // 2
            halves = [slice(0, width), slice(width, CHUNK)]
            rounded = [z_bf[LAST][:, PACK * cols.start : PACK * cols.stop] for cols in halves]
            for cols, dst in zip(halves, rounded):
                interleave(nc.vector.tensor_copy, dst, z_planes[LAST][:, :, cols])
            z_codes, z_bytes = quantised_tiles(LAST)
            banks = {}
            for half, (cols, src) in enumerate(zip(halves, rounded)):
                nc.vector.quantize_mx(out=z_codes[:, cols].bitcast(FP8X4), scales=z_bytes[:, cols], in_=src)
                for m in range(ROW_TILES):
                    banks[half, m] = psum.tile([P, width], F32, name="acc", tag="bank%d" % (ROW_TILES * half + m))
                    product(nc, banks[half, m][:], w2_codes, w2_bytes, m, z_codes[:, cols], z_bytes[:, cols])
            for half, cols in enumerate(halves):
                first = LAST * CHUNK + cols.start
                for m in range(0, ROW_TILES, 2):
                    staged = keep.tile([P, 2, width], F32, name="staged_last%d_%d" % (half, m))
                    nc.scalar.copy(out=staged[:, 0, :], in_=banks[half, m][:])
                    nc.vector.tensor_copy(out=staged[:, 1, :], in_=banks[half, m + 1][:])
                    nc.sync.dma_start(out_rows[:, m : m + 2, first : first + width], staged[:])

        for c in range(LAST):
            if c >= 2:
                project(c - 2)
            for t in range(PACK):
                difference(c, t)
            interleave(nc.scalar.copy, z_bf[c], z_planes[c])

        project(LAST - 2)
        for t in LAST_PLANE_ORDER[:2]:
            difference(LAST, t)
        project(LAST - 1)
        for t in LAST_PLANE_ORDER[2:]:
            difference(LAST, t)
        finish_last()
